import numpy as np
CORES = [4,5,6,7,12,13,14,15,132,133,134,135,140,141,142,143]
N = 16
def setup_inputs(rng):
    return {"x": rng.standard_normal((N, 128, 128), dtype=np.float32)}
def reference(x):
    b = 128 // N
    blocks = x.reshape(N, 128, N, b)
    return {"y": np.ascontiguousarray(blocks.transpose(2, 1, 0, 3)).reshape(N, 128, 128)}

@@ -1,0 +1,96 @@
+from concourse.bass import DstId, RemoteDMATransfer
+import comms_topo
+
+SCRATCH = {
+    "xs": ("sbuf", [128, 128], "float32"),
+    "land": ("sbuf", [128, 128], "float32"),
+    "st": ("sbuf", [128, 64], "float32"),
+}
+SEMAPHORES = ["loaded", "arrived", "in0", "in1", "sent", "stored"]
+
+CACHE = {}
+PAIRS_LO = [0x0003, 0x000C, 0x0030, 0x00C0]
+PAIRS_HI = [0x0300, 0x0C00, 0x3000, 0xC000]
+THREE_HI = [0x0F00, 0x3000, 0xC000]
+
+
+def bits(m):
+    return bin(m).count("1")
+
+
+def build_plan(cores):
+    base = [cores[4 * q] - 4 for q in range(4)]
+    prog, total = {}, {}
+
+    def call(core, transfers):
+        prog.setdefault(core, []).append(("call", transfers))
+        for t in transfers:
+            total[(t[3], t[7])] = total.get((t[3], t[7]), 0) + bits(t[6])
+            total[(core, "sent")] = total.get((core, "sent"), 0) + bits(t[6])
+
+    def wait(core, sem):
+        prog.setdefault(core, []).append(("wait", sem))
+
+    def spread(core, slot, src_rank, q_dst, masks):
+        wait(core, "in%d" % slot)
+        call(core, [("st", 32 * slot + 8 * m, 8, base[q_dst] + 4 + m, "land", 8 * src_rank, masks[m], "arrived")
+                    for m in range(4)])
+
+    def siblings(q, k):
+        return [("xs", 8 * (4 * q + m), 8, base[q] + 4 + m, "land", 8 * (4 * q + k), THREE_HI[i], "arrived")
+                for i, m in enumerate([m for m in range(4) if m != k])]
+
+    for q in range(4):
+        b = base[q]
+        mate, plane, diag = q ^ 1, q ^ 2, q ^ 3
+        for k in (0, 1):
+            r, c = 4 * q + k, b + 4 + k
+            call(c, [("xs", 32 * mate, 32, b + 2 + k, "st", 0, 0x00FF, "in0"),
+                     ("xs", 32 * diag, 32, b + 6 + k, "st", 0, 0xFF00, "in0")])
+            call(c, [("xs", 8 * (4 * plane + m), 8, base[plane] + 4 + m, "land", 8 * r, PAIRS_LO[m], "arrived")
+                     for m in range(4)] + siblings(q, k))
+        for k in (2, 3):
+            r, c = 4 * q + k, b + 4 + k
+            call(c, [("xs", 32 * mate, 32, base[mate] + k - 2, "st", 32, 0x000F, "in1"),
+                     ("xs", 32 * diag, 32, base[diag] + k, "st", 32, 0x00F0, "in1"),
+                     ("xs", 32 * plane, 32, b + k - 2, "st", 0, 0xFF00, "in0")])
+            call(c, siblings(q, k))
+            spread(c, 0, 4 * q + k - 2, diag, PAIRS_LO)
+        for i in (0, 1):
+            spread(b + i, 0, 4 * q + 2 + i, plane, PAIRS_LO)
+            spread(b + i, 1, 4 * mate + 2 + i, q, PAIRS_HI)
+            spread(b + 2 + i, 0, 4 * q + i, mate, PAIRS_LO)
+            spread(b + 2 + i, 1, 4 * diag + 2 + i, q, PAIRS_HI)
+    return {"prog": prog, "total": total}
+
+
+def rank_program(g, core, T, topo):
+    key = tuple(T.cores)
+    if key not in CACHE:
+        CACHE[key] = build_plan(list(T.cores))
+    plan = CACHE[key]
+    ops = plan["prog"].get(core)
+    if ops is None:
+        return
+    total = plan["total"]
+    rank = T.rank_of(core)
+    if rank is not None:
+        c0 = 8 * rank
+        g.sync.dma_start(T.xs[:, :], T.x[:, :]).then_inc(T.sem.loaded, 16)
+        g.scalar.dma_start(T.land[:, c0:c0 + 8], T.x[:, c0:c0 + 8]).then_inc(T.sem.arrived, 16)
+        g.sync.wait_ge(T.sem.arrived, total[(core, "arrived")] + 16)
+        g.sync.dma_start(T.y[:, :], T.land[:, :]).then_inc(T.sem.stored, 16)
+        g.wait_ge(T.sem.loaded, 16)
+    for op in ops:
+        if op[0] == "wait":
+            g.wait_ge(T.sem[op[1]], total[(core, op[1])])
+            continue
+        trs = []
+        for (sb, s0, w, dc, db, d0, mask, sem) in op[1]:
+            rid, pid = topo.addr(dc, core)
+            trs.append(RemoteDMATransfer(dst_ids=[DstId(rid=rid, pnc=pid)], dma_engine_mask=mask, remote_sem=T.sem[sem],
+                                         src=T[sb][:, s0:s0 + w], dst=T[db][:, d0:d0 + w]))
+        g.remote_dma_fused(trs, local_sem=T.sem.sent)
+    g.wait_ge(T.sem.sent, total[(core, "sent")])
+    if rank is not None:
+        g.wait_ge(T.sem.stored, 16)

@@ -8,7 +8,11 @@ SCRATCH = {
 }
 SEMAPHORES = ["loaded", "arrived", "in0", "in1", "sent", "stored"]
 
+SPLIT_P = True
+SWAP = False
+
 CACHE = {}
+LO, HI = 0x00FF, 0xFF00
 PAIRS_LO = [0x0003, 0x000C, 0x0030, 0x00C0]
 PAIRS_HI = [0x0300, 0x0C00, 0x3000, 0xC000]
 THREE_HI = [0x0F00, 0x3000, 0xC000]
@@ -31,36 +35,42 @@ def build_plan(cores):
     def wait(core, sem):
         prog.setdefault(core, []).append(("wait", sem))
 
+    def piece(q_dst, to, slot, mask):
+        return ("xs", 32 * q_dst, 32, to, "st", 32 * slot, mask, "in%d" % slot)
+
+    def blocks(buf, col, src_rank, q_dst, masks, skip=None):
+        ms = [m for m in range(4) if m != skip]
+        return [(buf, col + 8 * m, 8, base[q_dst] + 4 + m, "land", 8 * src_rank, masks[i], "arrived")
+                for i, m in enumerate(ms)]
+
     def spread(core, slot, src_rank, q_dst, masks):
         wait(core, "in%d" % slot)
-        call(core, [("st", 32 * slot + 8 * m, 8, base[q_dst] + 4 + m, "land", 8 * src_rank, masks[m], "arrived")
-                    for m in range(4)])
-
-    def siblings(q, k):
-        return [("xs", 8 * (4 * q + m), 8, base[q] + 4 + m, "land", 8 * (4 * q + k), THREE_HI[i], "arrived")
-                for i, m in enumerate([m for m in range(4) if m != k])]
+        call(core, blocks("st", 32 * slot, src_rank, q_dst, masks))
 
     for q in range(4):
         b = base[q]
         mate, plane, diag = q ^ 1, q ^ 2, q ^ 3
+        by_helper, by_rank = (diag, mate) if SWAP else (mate, diag)
         for k in (0, 1):
             r, c = 4 * q + k, b + 4 + k
-            call(c, [("xs", 32 * mate, 32, b + 2 + k, "st", 0, 0x00FF, "in0"),
-                     ("xs", 32 * diag, 32, b + 6 + k, "st", 0, 0xFF00, "in0")])
-            call(c, [("xs", 8 * (4 * plane + m), 8, base[plane] + 4 + m, "land", 8 * r, PAIRS_LO[m], "arrived")
-                     for m in range(4)] + siblings(q, k))
+            call(c, [piece(by_helper, b + 2 + k, 0, LO), piece(by_rank, b + 6 + k, 0, HI)])
+            call(c, blocks("xs", 32 * plane, r, plane, PAIRS_LO) + blocks("xs", 32 * q, r, q, THREE_HI, skip=k))
+            spread(b + 2 + k, 0, r, by_helper, PAIRS_LO)
         for k in (2, 3):
             r, c = 4 * q + k, b + 4 + k
-            call(c, [("xs", 32 * mate, 32, base[mate] + k - 2, "st", 32, 0x000F, "in1"),
-                     ("xs", 32 * diag, 32, base[diag] + k, "st", 32, 0x00F0, "in1"),
-                     ("xs", 32 * plane, 32, b + k - 2, "st", 0, 0xFF00, "in0")])
-            call(c, siblings(q, k))
-            spread(c, 0, 4 * q + k - 2, diag, PAIRS_LO)
-        for i in (0, 1):
-            spread(b + i, 0, 4 * q + 2 + i, plane, PAIRS_LO)
-            spread(b + i, 1, 4 * mate + 2 + i, q, PAIRS_HI)
-            spread(b + 2 + i, 0, 4 * q + i, mate, PAIRS_LO)
-            spread(b + 2 + i, 1, 4 * diag + 2 + i, q, PAIRS_HI)
+            if SPLIT_P:
+                call(c, [piece(diag, base[diag] + k, 1, LO), piece(plane, b + k - 2, 0, HI)])
+                call(c, [piece(mate, base[mate] + k - 2, 1, LO)])
+            else:
+                call(c, [piece(mate, base[mate] + k - 2, 1, 0x000F), piece(diag, base[diag] + k, 1, 0x00F0),
+                         piece(plane, b + k - 2, 0, HI)])
+            call(c, blocks("xs", 32 * q, r, q, THREE_HI, skip=k))
+            spread(c, 0, r - 2, by_rank, PAIRS_LO)
+            spread(b + k - 2, 0, r, plane, PAIRS_LO)
+    for q in range(4):
+        for k in (2, 3):
+            spread(base[q] + k - 2, 1, 4 * (q ^ 1) + k, q, PAIRS_HI)
+            spread(base[q] + k, 1, 4 * (q ^ 3) + k, q, PAIRS_HI)
     return {"prog": prog, "total": total}
 
 

@@ -6,16 +6,13 @@ SCRATCH = {
     "land": ("sbuf", [128, 128], "float32"),
     "st": ("sbuf", [128, 64], "float32"),
 }
-SEMAPHORES = ["loaded", "arrived", "in0", "in1", "sent", "stored"]
-
-SPLIT_P = True
-SWAP = False
+SEMAPHORES = ["loaded", "arrived", "in0", "in1", "in2", "sent", "stored"]
 
 CACHE = {}
 LO, HI = 0x00FF, 0xFF00
 PAIRS_LO = [0x0003, 0x000C, 0x0030, 0x00C0]
-PAIRS_HI = [0x0300, 0x0C00, 0x3000, 0xC000]
 THREE_HI = [0x0F00, 0x3000, 0xC000]
+QUADS = [0x000F, 0x00F0, 0x0F00, 0xF000]
 
 
 def bits(m):
@@ -38,6 +35,9 @@ def build_plan(cores):
     def piece(q_dst, to, slot, mask):
         return ("xs", 32 * q_dst, 32, to, "st", 32 * slot, mask, "in%d" % slot)
 
+    def half(q_dst, h, to, col, mask, sem):
+        return ("xs", 32 * q_dst + 16 * h, 16, to, "st", col, mask, sem)
+
     def blocks(buf, col, src_rank, q_dst, masks, skip=None):
         ms = [m for m in range(4) if m != skip]
         return [(buf, col + 8 * m, 8, base[q_dst] + 4 + m, "land", 8 * src_rank, masks[i], "arrived")
@@ -47,30 +47,33 @@ def build_plan(cores):
         wait(core, "in%d" % slot)
         call(core, blocks("st", 32 * slot, src_rank, q_dst, masks))
 
+    def relay(core, sem, col, src_rank, q_dst, h):
+        wait(core, sem)
+        call(core, [("st", col + 8 * i, 8, base[q_dst] + 4 + 2 * h + i, "land", 8 * src_rank, QUADS[i], "arrived")
+                    for i in range(2)])
+
     for q in range(4):
         b = base[q]
         mate, plane, diag = q ^ 1, q ^ 2, q ^ 3
-        by_helper, by_rank = (diag, mate) if SWAP else (mate, diag)
+        for k in (2, 3):
+            r, c = 4 * q + k, b + 4 + k
+            call(c, [piece(diag, base[diag] + k - 2, 1, LO), piece(plane, b + k - 2, 0, HI)])
+            call(c, [piece(mate, base[mate] + k, 1, LO)])
+            call(c, blocks("xs", 32 * q, r, q, THREE_HI, skip=k))
+            spread(b + k - 2, 0, r, plane, PAIRS_LO)
         for k in (0, 1):
             r, c = 4 * q + k, b + 4 + k
-            call(c, [piece(by_helper, b + 2 + k, 0, LO), piece(by_rank, b + 6 + k, 0, HI)])
+            owners = (b + 2 + k, b + 6 + k)
+            call(c, [half(diag, h, owners[h], 0, (LO, HI)[h], "in0") for h in (0, 1)])
+            call(c, [half(mate, h, owners[h], 16, (LO, HI)[h], "in2") for h in (0, 1)])
             call(c, blocks("xs", 32 * plane, r, plane, PAIRS_LO) + blocks("xs", 32 * q, r, q, THREE_HI, skip=k))
-            spread(b + 2 + k, 0, r, by_helper, PAIRS_LO)
-        for k in (2, 3):
-            r, c = 4 * q + k, b + 4 + k
-            if SPLIT_P:
-                call(c, [piece(diag, base[diag] + k, 1, LO), piece(plane, b + k - 2, 0, HI)])
-                call(c, [piece(mate, base[mate] + k - 2, 1, LO)])
-            else:
-                call(c, [piece(mate, base[mate] + k - 2, 1, 0x000F), piece(diag, base[diag] + k, 1, 0x00F0),
-                         piece(plane, b + k - 2, 0, HI)])
-            call(c, blocks("xs", 32 * q, r, q, THREE_HI, skip=k))
-            spread(c, 0, r - 2, by_rank, PAIRS_LO)
-            spread(b + k - 2, 0, r, plane, PAIRS_LO)
+            for h in (0, 1):
+                relay(owners[h], "in0", 0, r, diag, h)
+                relay(owners[h], "in2", 16, r, mate, h)
     for q in range(4):
         for k in (2, 3):
-            spread(base[q] + k - 2, 1, 4 * (q ^ 1) + k, q, PAIRS_HI)
-            spread(base[q] + k, 1, 4 * (q ^ 3) + k, q, PAIRS_HI)
+            spread(base[q] + k - 2, 1, 4 * (q ^ 3) + k, q, QUADS)
+            spread(base[q] + k, 1, 4 * (q ^ 1) + k, q, QUADS)
     return {"prog": prog, "total": total}
 
 

@@ -6,7 +6,7 @@ SCRATCH = {
     "land": ("sbuf", [128, 128], "float32"),
     "st": ("sbuf", [128, 64], "float32"),
 }
-SEMAPHORES = ["loaded", "arrived", "in0", "in1", "in2", "sent", "stored"]
+SEMAPHORES = ["loaded", "loaded2", "arrived", "in0", "in1", "in2", "sent", "stored"]
 
 CACHE = {}
 LO, HI = 0x00FF, 0xFF00
@@ -89,7 +89,10 @@ def rank_program(g, core, T, topo):
     rank = T.rank_of(core)
     if rank is not None:
         c0 = 8 * rank
-        g.sync.dma_start(T.xs[:, :], T.x[:, :]).then_inc(T.sem.loaded, 16)
+        far = 64 * (1 - rank // 8)
+        near = 64 - far
+        g.sync.dma_start(T.xs[:, far:far + 64], T.x[:, far:far + 64]).then_inc(T.sem.loaded, 16)
+        g.sync.dma_start(T.xs[:, near:near + 64], T.x[:, near:near + 64]).then_inc(T.sem.loaded2, 16)
         g.scalar.dma_start(T.land[:, c0:c0 + 8], T.x[:, c0:c0 + 8]).then_inc(T.sem.arrived, 16)
         g.sync.wait_ge(T.sem.arrived, total[(core, "arrived")] + 16)
         g.sync.dma_start(T.y[:, :], T.land[:, :]).then_inc(T.sem.stored, 16)
@@ -104,6 +107,8 @@ def rank_program(g, core, T, topo):
             trs.append(RemoteDMATransfer(dst_ids=[DstId(rid=rid, pnc=pid)], dma_engine_mask=mask, remote_sem=T.sem[sem],
                                          src=T[sb][:, s0:s0 + w], dst=T[db][:, d0:d0 + w]))
         g.remote_dma_fused(trs, local_sem=T.sem.sent)
+        if rank is not None and op is ops[0]:
+            g.wait_ge(T.sem.loaded2, 16)
     g.wait_ge(T.sem.sent, total[(core, "sent")])
     if rank is not None:
         g.wait_ge(T.sem.stored, 16)

from concourse.bass import DstId, RemoteDMATransfer
import comms_topo

SCRATCH = {
    "xs": ("sbuf", [128, 128], "float32"),
    "land": ("sbuf", [128, 128], "float32"),
    "st": ("sbuf", [128, 64], "float32"),
}
SEMAPHORES = ["loaded", "loaded2", "arrived", "in0", "in1", "in2", "sent", "stored"]

CACHE = {}
LO, HI = 0x00FF, 0xFF00
PAIRS_LO = [0x0003, 0x000C, 0x0030, 0x00C0]
THREE_HI = [0x0F00, 0x3000, 0xC000]
QUADS = [0x000F, 0x00F0, 0x0F00, 0xF000]


def bits(m):
    return bin(m).count("1")


def build_plan(cores):
    base = [cores[4 * q] - 4 for q in range(4)]
    prog, total = {}, {}

    def call(core, transfers):
        prog.setdefault(core, []).append(("call", transfers))
        for t in transfers:
            total[(t[3], t[7])] = total.get((t[3], t[7]), 0) + bits(t[6])
            total[(core, "sent")] = total.get((core, "sent"), 0) + bits(t[6])

    def wait(core, sem):
        prog.setdefault(core, []).append(("wait", sem))

    def piece(q_dst, to, slot, mask):
        return ("xs", 32 * q_dst, 32, to, "st", 32 * slot, mask, "in%d" % slot)

    def half(q_dst, h, to, col, mask, sem):
        return ("xs", 32 * q_dst + 16 * h, 16, to, "st", col, mask, sem)

    def blocks(buf, col, src_rank, q_dst, masks, skip=None):
        ms = [m for m in range(4) if m != skip]
        return [(buf, col + 8 * m, 8, base[q_dst] + 4 + m, "land", 8 * src_rank, masks[i], "arrived")
                for i, m in enumerate(ms)]

    def spread(core, slot, src_rank, q_dst, masks):
        wait(core, "in%d" % slot)
        call(core, blocks("st", 32 * slot, src_rank, q_dst, masks))

    def relay(core, sem, col, src_rank, q_dst, h):
        wait(core, sem)
        call(core, [("st", col + 8 * i, 8, base[q_dst] + 4 + 2 * h + i, "land", 8 * src_rank, QUADS[i], "arrived")
                    for i in range(2)])

    for q in range(4):
        b = base[q]
        mate, plane, diag = q ^ 1, q ^ 2, q ^ 3
        for k in (2, 3):
            r, c = 4 * q + k, b + 4 + k
            call(c, [piece(diag, base[diag] + k - 2, 1, LO), piece(plane, b + k - 2, 0, HI)])
            call(c, [piece(mate, base[mate] + k, 1, LO)])
            call(c, blocks("xs", 32 * q, r, q, THREE_HI, skip=k))
            spread(b + k - 2, 0, r, plane, PAIRS_LO)
        for k in (0, 1):
            r, c = 4 * q + k, b + 4 + k
            owners = (b + 2 + k, b + 6 + k)
            call(c, [half(diag, h, owners[h], 0, (LO, HI)[h], "in0") for h in (0, 1)])
            call(c, [half(mate, h, owners[h], 16, (LO, HI)[h], "in2") for h in (0, 1)])
            call(c, blocks("xs", 32 * plane, r, plane, PAIRS_LO) + blocks("xs", 32 * q, r, q, THREE_HI, skip=k))
            for h in (0, 1):
                relay(owners[h], "in0", 0, r, diag, h)
                relay(owners[h], "in2", 16, r, mate, h)
    for q in range(4):
        for k in (2, 3):
            spread(base[q] + k - 2, 1, 4 * (q ^ 3) + k, q, QUADS)
            spread(base[q] + k, 1, 4 * (q ^ 1) + k, q, QUADS)
    return {"prog": prog, "total": total}


def rank_program(g, core, T, topo):
    key = tuple(T.cores)
    if key not in CACHE:
        CACHE[key] = build_plan(list(T.cores))
    plan = CACHE[key]
    ops = plan["prog"].get(core)
    if ops is None:
        return
    total = plan["total"]
    rank = T.rank_of(core)
    if rank is not None:
        c0 = 8 * rank
        far = 64 * (1 - rank // 8)
        near = 64 - far
        g.sync.dma_start(T.xs[:, far:far + 64], T.x[:, far:far + 64]).then_inc(T.sem.loaded, 16)
        g.sync.dma_start(T.xs[:, near:near + 64], T.x[:, near:near + 64]).then_inc(T.sem.loaded2, 16)
        g.scalar.dma_start(T.land[:, c0:c0 + 8], T.x[:, c0:c0 + 8]).then_inc(T.sem.arrived, 16)
        g.sync.wait_ge(T.sem.arrived, total[(core, "arrived")] + 16)
        g.sync.dma_start(T.y[:, :], T.land[:, :]).then_inc(T.sem.stored, 16)
        g.wait_ge(T.sem.loaded, 16)
    for op in ops:
        if op[0] == "wait":
            g.wait_ge(T.sem[op[1]], total[(core, op[1])])
            continue
        trs = []
        for (sb, s0, w, dc, db, d0, mask, sem) in op[1]:
            rid, pid = topo.addr(dc, core)
            trs.append(RemoteDMATransfer(dst_ids=[DstId(rid=rid, pnc=pid)], dma_engine_mask=mask, remote_sem=T.sem[sem],
                                         src=T[sb][:, s0:s0 + w], dst=T[db][:, d0:d0 + w]))
        g.remote_dma_fused(trs, local_sem=T.sem.sent)
        if rank is not None and op is ops[0]:
            g.wait_ge(T.sem.loaded2, 16)
    g.wait_ge(T.sem.sent, total[(core, "sent")])
    if rank is not None:
        g.wait_ge(T.sem.stored, 16)
